import numpy as np
import ml_dtypes


def mxq(x, axis, fmt="e4m3"):
    dtype, down = {"e4m3": (ml_dtypes.float8_e4m3fn, 7), "e5m2": (ml_dtypes.float8_e5m2, 14)}[fmt]
    v = np.moveaxis(np.asarray(x, np.float32).astype(ml_dtypes.bfloat16).astype(np.float64), axis, -1)
    blocks = v.reshape(v.shape[:-1] + (-1, 32))
    amax = np.abs(blocks).max(-1, keepdims=True)
    byte = np.maximum(np.where(amax > 0, np.frexp(amax)[1] - 1 + 127, 0) - down, 1)
    scale = np.exp2(byte - 127.0)
    codes = (blocks / scale).astype(np.float32).astype(dtype).astype(np.float64)
    return np.moveaxis((codes * scale).reshape(v.shape), -1, axis)


WIDE = False


def mx_kscale(k):
    if not WIDE:
        return np.ones(k)
    levels = np.array([10, -10, 5, -5, 0])
    if k % 512:
        return np.exp2(np.random.permutation(np.resize(levels, k // 32))).repeat(32)
    a = np.empty((k // 512, 16))
    for p in range(k // 512):
        a[p, :8] = np.random.permutation(np.resize(levels, 8))
        for g in range(8):
            far = levels[np.abs(levels - a[p, g]) >= 10]
            a[p, g + 8] = far[np.random.randint(len(far))]
    return np.exp2(a.ravel()).repeat(32)


BF16 = ml_dtypes.bfloat16


def bf(x):
    return np.asarray(x, np.float32).astype(BF16)


def f64(x):
    return np.asarray(x).astype(np.float64)


E2M1 = np.array([0.0, 0.5, 1.0, 1.5, 2.0, 3.0, 4.0, 6.0, -0.0, -0.5, -1.0, -1.5, -2.0, -3.0, -4.0, -6.0])


def pack_weight(w, fmt):
    k, n = w.shape
    w = f64(bf(w)).reshape(k // 32, 32, n)
    amax = np.abs(w).max(1)
    if fmt == "e4m3":
        byte = np.frexp(amax)[1] - 1 + 127 - 7
    else:
        mant, ex = np.frexp(amax / 6.0)
        byte = np.where(mant > 0.5, ex, ex - 1) + 127
    byte = np.clip(np.where(amax > 0, byte, 1), 1, 254)
    scaled = (w * np.exp2(127.0 - byte)[:, None, :]).reshape(k, n).astype(np.float32)
    by_word = np.ascontiguousarray(scaled.reshape(k // 512, 128, 4, n).transpose(0, 1, 3, 2))
    if fmt == "e4m3":
        words = by_word.astype(ml_dtypes.float8_e4m3fn).view(np.uint8)
    else:
        c = by_word.astype(ml_dtypes.float4_e2m1fn).view(np.uint8) & 0xF
        words = c[..., 0::2] | (c[..., 1::2] << 4)
    return np.ascontiguousarray(words), np.ascontiguousarray(byte.astype(np.uint8).reshape(k // 512, 16, n))


def unpack_weight(words, scales, fmt):
    g, p, n, _ = words.shape
    if fmt == "e4m3":
        vals = np.ascontiguousarray(words).view(ml_dtypes.float8_e4m3fn).astype(np.float64)
    else:
        nib = np.empty((g, p, n, 4), np.uint8)
        nib[..., 0::2] = words & 0xF
        nib[..., 1::2] = words >> 4
        vals = E2M1[nib]
    vals = vals * np.repeat(np.exp2(scales.astype(np.float64) - 127.0), 8, axis=1)[..., None]
    return vals.transpose(0, 1, 3, 2).reshape(g * 512, n)
def pack4(w):
    words, scales = pack_weight(w, "e2m1")
    return words.reshape(words.shape[0], 128, -1), scales


def unpack4(words, scales):
    return unpack_weight(words.reshape(words.shape[0], 128, -1, 2), scales, "e2m1")


def planes(Y):
    n, m = Y.shape
    b = f64(bf(Y)).reshape(n // 32, 32, m)
    amax = np.abs(b).max(1)
    byte = np.clip(np.where(amax > 0, np.frexp(amax)[1] - 1 + 127 - 7, 1), 1, 254)
    codes = (b * np.exp2(127.0 - byte)[:, None, :]).reshape(n, m).astype(np.float32).astype(ml_dtypes.float8_e4m3fn).view(np.uint8)
    words = codes.reshape(n // 512, 128, 4, m).transpose(0, 1, 3, 2)
    return np.ascontiguousarray(words), np.ascontiguousarray(byte.astype(np.uint8).reshape(n // 512, 16, m))


N = 1024


def setup_inputs():
    s = mx_kscale(N)
    t = mx_kscale(N)
    q, _ = np.linalg.qr(np.random.randn(N, N))
    base = q / np.sqrt(N)
    update = 0.35 * np.random.randn(N, N) / N
    inverse = q.T * np.sqrt(N)
    ts = t[:, None] * s[None, :]
    b_words, b_scales = pack4(np.ascontiguousarray((base * ts).T))
    return {
        "b_words": b_words,
        "b_scales": b_scales,
        "U": bf(update * ts),
        "X": bf(inverse / ts.T),
        "d_c": bf(np.exp(0.3 * np.random.randn(N)) * s),
        "d_r": bf(np.exp(0.8 * np.random.randn(N)) * t),
    }


def reference(b_words, b_scales, U, X, d_c, d_r):
    B = unpack4(b_words, b_scales)
    x_rows = mxq(f64(X), 0, "e4m3")
    x_cols = mxq(f64(X), 1, "e4m3")
    P = (mxq(f64(U), 1, "e4m3") @ x_rows) + (B.T @ x_rows)
    R = 2.0 * np.eye(N) - P
    Z = x_cols @ mxq(R, 0, "e4m3")
    y = f64(d_c)[:, None] * Z * f64(d_r)[None, :]
    Y = y.T
    words, scales = planes(Y)
    return y, words, scales

@@ -1,0 +1,395 @@
+from contextlib import ExitStack
+
+import concourse.mybir as mybir
+from concourse.masks import make_identity
+
+N = 1024
+FLOPS = 3 * 2 * N * N * N
+
+F32 = mybir.dt.float32
+BF16 = mybir.dt.bfloat16
+I32 = mybir.dt.int32
+U32 = mybir.dt.uint32
+U8 = mybir.dt.uint8
+FP8X4 = mybir.dt.float8_e4m3fn_x4
+FP4X4 = mybir.dt.float4_e2m1fn_x4
+ALU = mybir.AluOpType
+
+P = 128
+HALF = 512
+PAIR = 256
+
+
+def tile_newton_inverse_refinement_k6_kernel(tc, b_words, b_scales, U, X, d_c, d_r, out_0, out_1, out_2):
+    nc = tc.nc
+    with ExitStack() as ctx:
+        keep = ctx.enter_context(tc.tile_pool(name="keep", bufs=1))
+        flow = ctx.enter_context(tc.tile_pool(name="flow", bufs=4))
+        acc_pool = ctx.enter_context(tc.psum_pool(name="acc", bufs=4))
+        turn_pool = ctx.enter_context(tc.psum_pool(name="turn", bufs=4))
+        ctx.enter_context(tc.manual_schedule())
+
+        def kept(name, shape, dtype):
+            return keep.tile(shape, dtype, name=name, align_bytes=64)
+
+        def mx_operand(name, width):
+            return kept(name + "_codes", [P, width], U32), kept(name + "_scales", [P, width], U8)
+
+        both = (0, 1)
+        x_raw = {(g, c): kept("x_raw%d%d" % (g, c), [P, 4, HALF], BF16) for g in both for c in both}
+        u_raw = {(ih, g): kept("u_raw%d%d" % (ih, g), [P, 4, HALF], BF16) for ih in both for g in both}
+        b_codes = {ih: kept("b_codes%d" % ih, [P, 2, 2 * HALF], U8) for ih in both}
+        b_plane = kept("b_plane", [P, 2, N], U8)
+        x_rows = {(g, c): mx_operand("x_rows%d%d" % (g, c), HALF) for g in both for c in both}
+        x_cols = {(g, c): mx_operand("x_cols%d%d" % (g, c), HALF) for g in both for c in both}
+        u_mx = {(ih, g): mx_operand("u_mx%d%d" % (ih, g), HALF) for ih in both for g in both}
+        r_mx = {(jh, ih): mx_operand("r_mx%d%d" % (jh, ih), HALF) for jh in both for ih in both}
+        y_scales = kept("y_scales", [P, 2, N], U8)
+        ident = kept("ident", [P, P], F32)
+        two_eye = kept("two_eye", [P, 2, 224, 2], BF16)
+        dc_raw = kept("dc_raw", [P, 4, 2], BF16)
+        dc_neg = kept("dc_neg", [P, 4, 2], F32)
+        dr_rows = kept("dr_rows", [P, N], BF16)
+
+        nc.vector.memset(b_plane[:].rearrange("p g n -> p (g n)").bitcast(I32), 0)
+        make_identity(nc, ident[:])
+        nc.gpsimd.memset(two_eye[:], 0.0)
+        nc.gpsimd.tensor_scalar(
+            out=two_eye[:, :, 96:128, :],
+            in0=ident[:].rearrange("p (w u e) -> p u w e", u=2, e=2),
+            scalar1=2.0, scalar2=0.0, op0=ALU.mult, op1=ALU.add,
+        )
+
+        def load_x(g, c):
+            rows = X[g * HALF:(g + 1) * HALF, c * HALF:(c + 1) * HALF]
+            nc.sync.dma_start(out=x_raw[g, c][:], in_=rows.rearrange("(p t) n -> p t n", t=4))
+
+        def load_u(ih, g):
+            rows = U[ih * HALF:(ih + 1) * HALF, g * HALF:(g + 1) * HALF]
+            nc.sync.dma_start(out=u_raw[ih, g][:], in_=rows.rearrange("(r p) n -> p r n", p=P))
+
+        def load_b(ih):
+            src = b_words[:, :, ih * 2 * HALF:(ih + 1) * 2 * HALF].bitcast(I32)
+            nc.sync.dma_start(out=b_codes[ih][:].bitcast(I32), in_=src.rearrange("g p n -> p g n"))
+
+        for q in range(4):
+            nc.scalar.dma_start(
+                out=b_plane[32 * q:32 * q + 4, :, :].bitcast(I32),
+                in_=b_scales[:, 4 * q:4 * q + 4, :].bitcast(I32).rearrange("g r n -> r g n"),
+            )
+        load_x(0, 0)
+        load_b(1)
+        load_u(1, 0)
+        load_x(1, 0)
+        load_u(1, 1)
+        load_b(0)
+        load_u(0, 0)
+        load_u(0, 1)
+        load_x(0, 1)
+        load_x(1, 1)
+        nc.sync.dma_start(out=dc_raw[:], in_=d_c.rearrange("(a p e) -> p a e", p=P, e=2))
+        nc.sync.dma_start(out=dr_rows[:], in_=d_r.partition_broadcast(P))
+
+        grouped = {}
+        accs = {}
+        r_turned = {}
+        y_sorted = {}
+        ys = {}
+        sorted_raw = {}
+
+        def staging(key, width):
+            if key not in grouped:
+                grouped[key] = flow.tile([P, width, 4], BF16, name="grouped%d" % width, bufs=8, align_bytes=64)
+            return grouped[key]
+
+        def quantize(key, codes, scales, cols=slice(None)):
+            nc.vector.quantize_mx(
+                out=codes.bitcast(FP8X4), scales=scales, in_=grouped[key][:, cols, :].rearrange("p c t -> p (c t)")
+            )
+
+        def interleave_x(g, c, cols=slice(0, HALF)):
+            dst = staging(("x_rows", g, c), HALF)
+            nc.vector.tensor_copy(
+                out=dst[:, cols, :].rearrange("p (c i) t -> p c t i", i=4),
+                in_=x_raw[g, c][:, :, cols].rearrange("p t (c i) -> p c t i", i=4),
+            )
+
+        def quantize_x_rows(g, c, cols=slice(0, HALF)):
+            quantize(("x_rows", g, c), x_rows[g, c][0][:, cols], x_rows[g, c][1][:, cols], cols)
+
+        def turn(sources):
+            bank = turn_pool.tile([P, 2, 2, P], F32, name="turn")
+            for a in both:
+                for u in both:
+                    nc.tensor.transpose(bank[:, a, u, :], sources(a, u), ident[:])
+            return bank
+
+        def words(tile):
+            return tile[:].rearrange("p c t -> p (c t)").bitcast(F32)
+
+        def sort_words(key, raw, on_vector=True):
+            dst = flow.tile([P, 4, 2, P], F32, name="sorted_raw", bufs=4, align_bytes=64)
+            sorted_raw[key] = dst
+            src = raw[:].bitcast(F32).rearrange("p r (w u) -> p r u w", u=2)
+            if on_vector:
+                nc.vector.tensor_copy(out=dst[:], in_=src)
+            else:
+                nc.scalar.copy(out=dst[:], in_=src)
+
+        def word_class(key, raw, r, u):
+            if key in sorted_raw:
+                return sorted_raw[key][:, r, u, :]
+            return raw[:].bitcast(F32)[:, r, u:PAIR:2]
+
+        def sort_u(ih, g, on_vector=True):
+            sort_words(("u", ih, g), u_raw[ih, g], on_vector)
+
+        def sort_x(g, c, on_vector=True):
+            sort_words(("x", g, c), x_raw[g, c], on_vector)
+
+        def turn_u(ih, g):
+            dst = staging(("u", ih, g), HALF)
+            for k in both:
+                bank = turn(lambda a, u: word_class(("u", ih, g), u_raw[ih, g], 2 * k + a, u))
+                nc.scalar.copy(
+                    out=words(dst)[:, k * HALF:(k + 1) * HALF].rearrange("p (a i u) -> p a i u", a=2, u=2),
+                    in_=bank[:].rearrange("p a u i -> p a i u"),
+                )
+
+        def quantize_u(ih, g):
+            quantize(("u", ih, g), u_mx[ih, g][0][:], u_mx[ih, g][1][:])
+
+        def turn_x(g, c):
+            dst = staging(("x_cols", g, c), HALF)
+            for e in both:
+                bank = turn(lambda a, u: word_class(("x", g, c), x_raw[g, c], e + 2 * a, u))
+                nc.scalar.copy(
+                    out=words(dst).rearrange("p (s e q a u) -> p s e q a u", s=2, e=2, a=2, u=2)[:, :, e, :, :, :],
+                    in_=bank[:].rearrange("p a u (s q) -> p s q a u", s=2),
+                )
+
+        def quantize_x_cols(g, c):
+            quantize(("x_cols", g, c), x_cols[g, c][0][:], x_cols[g, c][1][:])
+
+        def first_pass(b, ih, g, base):
+            first = base and g == 0
+            if first:
+                accs[b, ih] = acc_pool.tile([P, HALF], F32, name="acc")
+            cols = slice(P * (b % 4), P * (b % 4 + 1))
+            codes, scales = x_rows[g, b // 4]
+            if base:
+                rhs = b_codes[ih][:, g, :].bitcast(FP4X4)
+                rhs_scale = b_plane[:, g, ih * HALF:(ih + 1) * HALF]
+            else:
+                rhs = u_mx[ih, g][0][:].bitcast(FP8X4)
+                rhs_scale = u_mx[ih, g][1][:]
+            nc.tensor.matmul_mx(
+                out=accs[b, ih][:], lhsT=codes[:, cols].bitcast(FP8X4), lhsT_scale=scales[:, cols],
+                rhs=rhs, rhs_scale=rhs_scale, start=first, stop=(g == 1 and not base),
+            )
+
+        def residual(b, ih):
+            dst = flow.tile([P, 2, P, 2], BF16, name="r_turned", bufs=8, align_bytes=64)
+            r_turned[b, ih] = dst
+            src = accs[b, ih][:].rearrange("p (w u e) -> p u w e", u=2, e=2)
+            if b // 4 == ih:
+                w0 = 96 - 32 * (b % 4)
+                nc.vector.tensor_tensor(out=dst[:], in0=src, in1=two_eye[:, :, w0:w0 + P, :], op=ALU.subtract)
+            else:
+                nc.scalar.copy(out=dst[:], in_=src)
+
+        def first_stage(b, ih):
+            for base in (True, False):
+                for g in both:
+                    first_pass(b, ih, g, base)
+            residual(b, ih)
+
+        def sorted_words(tile, u):
+            return tile[:].rearrange("p u w e -> p u (w e)").bitcast(F32)[:, u, :]
+
+        def turn_r(bp, ih):
+            dst = staging(("r", bp, ih), PAIR)
+            bank = turn(lambda a, u: sorted_words(r_turned[2 * bp + a, ih], u))
+            nc.scalar.copy(
+                out=words(dst).rearrange("p (a j u) -> p a j u", a=2, u=2),
+                in_=bank[:].rearrange("p a u j -> p a j u"),
+            )
+
+        def quantize_r(bp, ih):
+            cols = slice(PAIR * (bp % 2), PAIR * (bp % 2 + 1))
+            codes, scales = r_mx[bp // 2, ih]
+            quantize(("r", bp, ih), codes[:, cols], scales[:, cols])
+
+        def second_pass(hp, e, jh, ih):
+            if ih == 0:
+                accs[hp, e, jh] = acc_pool.tile([P, HALF], F32, name="acc")
+            c0 = PAIR * (hp % 2) + P * e
+            codes, scales = x_cols[hp // 2, ih]
+            nc.tensor.matmul_mx(
+                out=accs[hp, e, jh][:], lhsT=codes[:, c0:c0 + P].bitcast(FP8X4), lhsT_scale=scales[:, c0:c0 + P],
+                rhs=r_mx[jh, ih][0][:].bitcast(FP8X4), rhs_scale=r_mx[jh, ih][1][:],
+                start=(ih == 0), stop=(ih == 1),
+            )
+
+        def second_stage(hp, e, jh):
+            if (hp, e, jh) not in accs:
+                second_pass(hp, e, jh, 0)
+            second_pass(hp, e, jh, 1)
+            scale_y(hp, e, jh)
+
+        def scale_y(hp, e, jh):
+            acc = accs[hp, e, jh]
+            y = flow.tile([P, HALF], F32, name="y", bufs=8, align_bytes=64)
+            nc.vector.scalar_tensor_tensor(
+                out=y[:], in0=acc[:], scalar=dc_neg[:, hp, e:e + 1], in1=dr_rows[:, jh * HALF:(jh + 1) * HALF],
+                op0=ALU.mult, op1=ALU.mult,
+            )
+            rows = out_0[hp * PAIR:(hp + 1) * PAIR, jh * HALF:(jh + 1) * HALF]
+            nc.sync.dma_start(out=rows.rearrange("(p e) n -> p e n", e=2)[:, e, :], in_=y[:])
+            ys[hp, e, jh] = y
+
+        def round_y(hp, e, jh, on_vector=False):
+            dst = flow.tile([P, 2, P, 2], BF16, name="y_sorted", bufs=8, align_bytes=64)
+            y_sorted[hp, e, jh] = dst
+            src = ys[hp, e, jh][:].rearrange("p (w u e) -> p u w e", u=2, e=2)
+            if on_vector:
+                nc.vector.tensor_copy(out=dst[:], in_=src)
+            else:
+                nc.scalar.copy(out=dst[:], in_=src)
+
+        def turn_y(hp, jh):
+            dst = staging(("y", hp, jh), PAIR)
+            bank = turn(lambda a, u: sorted_words(y_sorted[hp, a, jh], u))
+            nc.scalar.copy(
+                out=words(dst).rearrange("p (m a u) -> p m a u", a=2, u=2),
+                in_=bank[:].rearrange("p a u m -> p m a u"),
+            )
+
+        def quantize_y(hp, jh):
+            codes = flow.tile([P, PAIR], U32, name="y_codes", bufs=8, align_bytes=64)
+            cols = slice(hp * PAIR, (hp + 1) * PAIR)
+            quantize(("y", hp, jh), codes[:], y_scales[:, jh, cols])
+            dst = out_1[jh].rearrange("p m t -> p (m t)").bitcast(I32)
+            nc.sync.dma_start(out=dst[:, cols], in_=codes[:].bitcast(I32))
+
+        def store_y_scales():
+            for q in range(4):
+                queue = nc.scalar if q % 2 else nc.sync
+                queue.dma_start(
+                    out=out_2[:, 4 * q:4 * q + 4, :].bitcast(I32).rearrange("g r n -> r g n"),
+                    in_=y_scales[32 * q:32 * q + 4, :, :].bitcast(I32),
+                )
+
+        def second_pair(hp, jh):
+            for e in both:
+                second_stage(hp, e, jh)
+                round_y(hp, e, jh)
+
+        def passes(ih, g, base):
+            for b in range(4):
+                first_pass(b, ih, g, base)
+
+        halves = (slice(0, PAIR), slice(PAIR, HALF))
+        for half in halves:
+            interleave_x(0, 0, half)
+            quantize_x_rows(0, 0, half)
+        turn_x(0, 0)
+        sort_u(1, 0)
+        passes(1, 0, True)
+        turn_u(1, 0)
+        turn_x(1, 0)
+        interleave_x(1, 0)
+        sort_u(1, 1)
+        quantize_x_rows(1, 0)
+        quantize_u(1, 0)
+        turn_u(1, 1)
+        passes(1, 1, True)
+        passes(1, 0, False)
+        sort_u(0, 0)
+        sort_u(0, 1)
+        quantize_u(1, 1)
+        turn_u(0, 0)
+        turn_u(0, 1)
+        interleave_x(0, 1)
+        quantize_u(0, 0)
+        for b in range(4):
+            first_pass(b, 1, 1, False)
+            residual(b, 1)
+        quantize_x_rows(0, 1)
+        quantize_u(0, 1)
+        sort_x(0, 1)
+        first_stage(0, 0)
+        interleave_x(1, 1)
+        first_stage(1, 0)
+        turn_r(0, 1)
+        turn_r(1, 1)
+        turn_x(0, 1)
+        quantize_x_rows(1, 1)
+        sort_x(1, 1)
+        first_stage(2, 0)
+        quantize_x_cols(0, 0)
+        quantize_r(0, 1)
+        first_stage(3, 0)
+        turn_r(0, 0)
+        turn_x(1, 1)
+        quantize_r(1, 1)
+        quantize_x_cols(0, 1)
+        nc.vector.tensor_scalar(out=dc_neg[:], in0=dc_raw[:], scalar1=-1.0, scalar2=None, op0=ALU.mult)
+        first_stage(4, 0)
+        turn_r(1, 0)
+        quantize_r(0, 0)
+        quantize_x_cols(1, 0)
+        first_stage(5, 0)
+        quantize_r(1, 0)
+        quantize_x_cols(1, 1)
+        second_pair(0, 0)
+        first_stage(4, 1)
+        turn_r(2, 0)
+        turn_y(0, 0)
+        second_pair(1, 0)
+        quantize_r(2, 0)
+        first_stage(5, 1)
+        quantize_y(0, 0)
+        first_stage(6, 0)
+        turn_y(1, 0)
+        turn_r(2, 1)
+        first_stage(7, 0)
+        quantize_y(1, 0)
+        quantize_r(2, 1)
+        second_pair(2, 0)
+        first_stage(6, 1)
+        turn_r(3, 0)
+        turn_y(2, 0)
+        first_stage(7, 1)
+        quantize_r(3, 0)
+        second_stage(3, 0, 0)
+        second_stage(3, 1, 0)
+        turn_r(3, 1)
+        quantize_y(2, 0)
+        round_y(3, 0, 0)
+        round_y(3, 1, 0, True)
+        quantize_r(3, 1)
+        for hp in both:
+            for e in both:
+                second_pass(hp, e, 1, 0)
+        turn_y(3, 0)
+        second_pair(0, 1)
+        second_pair(1, 1)
+        second_stage(2, 0, 1)
+        second_stage(2, 1, 1)
+        turn_y(0, 1)
+        round_y(2, 0, 1)
+        second_stage(3, 0, 1)
+        second_stage(3, 1, 1)
+        turn_y(1, 1)
+        round_y(2, 1, 1, True)
+        round_y(3, 0, 1)
+        round_y(3, 1, 1, True)
+        quantize_y(3, 0)
+        quantize_y(0, 1)
+        turn_y(2, 1)
+        quantize_y(1, 1)
+        turn_y(3, 1)
+        quantize_y(2, 1)
+        quantize_y(3, 1)
+        store_y_scales()

@@ -43,7 +43,7 @@ def tile_newton_inverse_refinement_k6_kernel(tc, b_words, b_scales, U, X, d_c, d
         x_rows = {(g, c): mx_operand("x_rows%d%d" % (g, c), HALF) for g in both for c in both}
         x_cols = {(g, c): mx_operand("x_cols%d%d" % (g, c), HALF) for g in both for c in both}
         u_mx = {(ih, g): mx_operand("u_mx%d%d" % (ih, g), HALF) for ih in both for g in both}
-        r_mx = {(jh, ih): mx_operand("r_mx%d%d" % (jh, ih), HALF) for jh in both for ih in both}
+        r_mx = {(jq, ih): mx_operand("r_mx%d%d" % (jq, ih), PAIR) for jq in range(4) for ih in both}
         y_scales = kept("y_scales", [P, 2, N], U8)
         ident = kept("ident", [P, P], F32)
         two_eye = kept("two_eye", [P, 2, 224, 2], BF16)
@@ -72,18 +72,21 @@ def tile_newton_inverse_refinement_k6_kernel(tc, b_words, b_scales, U, X, d_c, d
             src = b_words[:, :, ih * 2 * HALF:(ih + 1) * 2 * HALF].bitcast(I32)
             nc.sync.dma_start(out=b_codes[ih][:].bitcast(I32), in_=src.rearrange("g p n -> p g n"))
 
-        for q in range(4):
-            nc.scalar.dma_start(
-                out=b_plane[32 * q:32 * q + 4, :, :].bitcast(I32),
-                in_=b_scales[:, 4 * q:4 * q + 4, :].bitcast(I32).rearrange("g r n -> r g n"),
-            )
+        def load_b_scales():
+            for q in range(4):
+                nc.sync.dma_start(
+                    out=b_plane[32 * q:32 * q + 4, :, :].bitcast(I32),
+                    in_=b_scales[:, 4 * q:4 * q + 4, :].bitcast(I32).rearrange("g r n -> r g n"),
+                )
+
         load_x(0, 0)
         load_b(1)
-        load_u(1, 0)
+        load_b_scales()
         load_x(1, 0)
+        load_u(1, 0)
         load_u(1, 1)
-        load_b(0)
         load_u(0, 0)
+        load_b(0)
         load_u(0, 1)
         load_x(0, 1)
         load_x(1, 1)
@@ -107,9 +110,9 @@ def tile_newton_inverse_refinement_k6_kernel(tc, b_words, b_scales, U, X, d_c, d
                 out=codes.bitcast(FP8X4), scales=scales, in_=grouped[key][:, cols, :].rearrange("p c t -> p (c t)")
             )
 
-        def interleave_x(g, c, cols=slice(0, HALF)):
+        def interleave_x(g, c, cols=slice(0, HALF), engine_copy=nc.vector.tensor_copy):
             dst = staging(("x_rows", g, c), HALF)
-            nc.vector.tensor_copy(
+            engine_copy(
                 out=dst[:, cols, :].rearrange("p (c i) t -> p c t i", i=4),
                 in_=x_raw[g, c][:, :, cols].rearrange("p t (c i) -> p c t i", i=4),
             )
@@ -159,11 +162,11 @@ def tile_newton_inverse_refinement_k6_kernel(tc, b_words, b_scales, U, X, d_c, d
         def quantize_u(ih, g):
             quantize(("u", ih, g), u_mx[ih, g][0][:], u_mx[ih, g][1][:])
 
-        def turn_x(g, c):
+        def turn_x(g, c, parities=both, engine_copy=nc.scalar.copy):
             dst = staging(("x_cols", g, c), HALF)
-            for e in both:
+            for e in parities:
                 bank = turn(lambda a, u: word_class(("x", g, c), x_raw[g, c], e + 2 * a, u))
-                nc.scalar.copy(
+                engine_copy(
                     out=words(dst).rearrange("p (s e q a u) -> p s e q a u", s=2, e=2, a=2, u=2)[:, :, e, :, :, :],
                     in_=bank[:].rearrange("p a u (s q) -> p s q a u", s=2),
                 )
@@ -188,7 +191,7 @@ def tile_newton_inverse_refinement_k6_kernel(tc, b_words, b_scales, U, X, d_c, d
                 rhs=rhs, rhs_scale=rhs_scale, start=first, stop=(g == 1 and not base),
             )
 
-        def residual(b, ih):
+        def residual(b, ih, engine_copy=nc.scalar.copy):
             dst = flow.tile([P, 2, P, 2], BF16, name="r_turned", bufs=8, align_bytes=64)
             r_turned[b, ih] = dst
             src = accs[b, ih][:].rearrange("p (w u e) -> p u w e", u=2, e=2)
@@ -196,7 +199,7 @@ def tile_newton_inverse_refinement_k6_kernel(tc, b_words, b_scales, U, X, d_c, d
                 w0 = 96 - 32 * (b % 4)
                 nc.vector.tensor_tensor(out=dst[:], in0=src, in1=two_eye[:, :, w0:w0 + P, :], op=ALU.subtract)
             else:
-                nc.scalar.copy(out=dst[:], in_=src)
+                engine_copy(out=dst[:], in_=src)
 
         def first_stage(b, ih):
             for base in (True, False):
@@ -205,62 +208,56 @@ def tile_newton_inverse_refinement_k6_kernel(tc, b_words, b_scales, U, X, d_c, d
             residual(b, ih)
 
         def sorted_words(tile, u):
-            return tile[:].rearrange("p u w e -> p u (w e)").bitcast(F32)[:, u, :]
+            return tile.rearrange("p u w e -> p u (w e)").bitcast(F32)[:, u, :]
 
         def turn_r(bp, ih):
             dst = staging(("r", bp, ih), PAIR)
-            bank = turn(lambda a, u: sorted_words(r_turned[2 * bp + a, ih], u))
+            bank = turn(lambda a, u: sorted_words(r_turned[2 * bp + a, ih][:], u))
             nc.scalar.copy(
                 out=words(dst).rearrange("p (a j u) -> p a j u", a=2, u=2),
                 in_=bank[:].rearrange("p a u j -> p a j u"),
             )
 
         def quantize_r(bp, ih):
-            cols = slice(PAIR * (bp % 2), PAIR * (bp % 2 + 1))
-            codes, scales = r_mx[bp // 2, ih]
-            quantize(("r", bp, ih), codes[:, cols], scales[:, cols])
+            codes, scales = r_mx[bp, ih]
+            quantize(("r", bp, ih), codes[:], scales[:])
 
-        def second_pass(hp, e, jh, ih):
-            if ih == 0:
-                accs[hp, e, jh] = acc_pool.tile([P, HALF], F32, name="acc")
-            c0 = PAIR * (hp % 2) + P * e
-            codes, scales = x_cols[hp // 2, ih]
-            nc.tensor.matmul_mx(
-                out=accs[hp, e, jh][:], lhsT=codes[:, c0:c0 + P].bitcast(FP8X4), lhsT_scale=scales[:, c0:c0 + P],
-                rhs=r_mx[jh, ih][0][:].bitcast(FP8X4), rhs_scale=r_mx[jh, ih][1][:],
-                start=(ih == 0), stop=(ih == 1),
+        def second_stage(hp, jq):
+            acc = acc_pool.tile([P, 2, PAIR], F32, name="acc")
+            for e in both:
+                c0 = PAIR * (hp % 2) + P * e
+                for ih in both:
+                    codes, scales = x_cols[hp // 2, ih]
+                    nc.tensor.matmul_mx(
+                        out=acc[:, e, :], lhsT=codes[:, c0:c0 + P].bitcast(FP8X4), lhsT_scale=scales[:, c0:c0 + P],
+                        rhs=r_mx[jq, ih][0][:].bitcast(FP8X4), rhs_scale=r_mx[jq, ih][1][:],
+                        start=(ih == 0), stop=(ih == 1),
+                    )
+            cols = slice(jq * PAIR, (jq + 1) * PAIR)
+            y = flow.tile([P, 2, PAIR], F32, name="y", bufs=8, align_bytes=64)
+            ys[hp, jq] = y
+            for e in both:
+                nc.vector.scalar_tensor_tensor(
+                    out=y[:, e, :], in0=acc[:, e, :], scalar=dc_neg[:, hp, e:e + 1], in1=dr_rows[:, cols],
+                    op0=ALU.mult, op1=ALU.mult,
+                )
+            rows = out_0[hp * PAIR:(hp + 1) * PAIR, cols]
+            nc.sync.dma_start(out=rows.rearrange("(p e) n -> p e n", e=2), in_=y[:])
+
+        def round_y(hp, jq, engine_copy=nc.scalar.copy):
+            jh = jq // 2
+            if (hp, jh) not in y_sorted:
+                y_sorted[hp, jh] = flow.tile([P, 2, 2, P, 2], BF16, name="y_sorted", bufs=8, align_bytes=64)
+            w0 = 64 * (jq % 2)
+            engine_copy(
+                out=y_sorted[hp, jh][:, :, :, w0:w0 + 64, :],
+                in_=ys[hp, jq][:].rearrange("p e (w u f) -> p e u w f", u=2, f=2),
             )
 
-        def second_stage(hp, e, jh):
-            if (hp, e, jh) not in accs:
-                second_pass(hp, e, jh, 0)
-            second_pass(hp, e, jh, 1)
-            scale_y(hp, e, jh)
-
-        def scale_y(hp, e, jh):
-            acc = accs[hp, e, jh]
-            y = flow.tile([P, HALF], F32, name="y", bufs=8, align_bytes=64)
-            nc.vector.scalar_tensor_tensor(
-                out=y[:], in0=acc[:], scalar=dc_neg[:, hp, e:e + 1], in1=dr_rows[:, jh * HALF:(jh + 1) * HALF],
-                op0=ALU.mult, op1=ALU.mult,
-            )
-            rows = out_0[hp * PAIR:(hp + 1) * PAIR, jh * HALF:(jh + 1) * HALF]
-            nc.sync.dma_start(out=rows.rearrange("(p e) n -> p e n", e=2)[:, e, :], in_=y[:])
-            ys[hp, e, jh] = y
-
-        def round_y(hp, e, jh, on_vector=False):
-            dst = flow.tile([P, 2, P, 2], BF16, name="y_sorted", bufs=8, align_bytes=64)
-            y_sorted[hp, e, jh] = dst
-            src = ys[hp, e, jh][:].rearrange("p (w u e) -> p u w e", u=2, e=2)
-            if on_vector:
-                nc.vector.tensor_copy(out=dst[:], in_=src)
-            else:
-                nc.scalar.copy(out=dst[:], in_=src)
-
-        def turn_y(hp, jh):
+        def turn_y(hp, jh, engine_copy=nc.scalar.copy):
             dst = staging(("y", hp, jh), PAIR)
-            bank = turn(lambda a, u: sorted_words(y_sorted[hp, a, jh], u))
-            nc.scalar.copy(
+            bank = turn(lambda a, u: sorted_words(y_sorted[hp, jh][:, a], u))
+            engine_copy(
                 out=words(dst).rearrange("p (m a u) -> p m a u", a=2, u=2),
                 in_=bank[:].rearrange("p a u m -> p m a u"),
             )
@@ -280,116 +277,126 @@ def tile_newton_inverse_refinement_k6_kernel(tc, b_words, b_scales, U, X, d_c, d
                     in_=y_scales[32 * q:32 * q + 4, :, :].bitcast(I32),
                 )
 
-        def second_pair(hp, jh):
-            for e in both:
-                second_stage(hp, e, jh)
-                round_y(hp, e, jh)
+        on_vector = nc.vector.tensor_copy
+        on_scalar = nc.scalar.copy
 
         def passes(ih, g, base):
             for b in range(4):
                 first_pass(b, ih, g, base)
 
-        halves = (slice(0, PAIR), slice(PAIR, HALF))
-        for half in halves:
-            interleave_x(0, 0, half)
-            quantize_x_rows(0, 0, half)
+        def second(hp, jq):
+            second_stage(hp, jq)
+            round_y(hp, jq)
+
+        low, high = slice(0, PAIR), slice(PAIR, HALF)
+        interleave_x(0, 0, low)
+        interleave_x(0, 0, high, on_scalar)
+        quantize_x_rows(0, 0, low)
+        quantize_x_rows(0, 0, high)
+        interleave_x(1, 0, high, on_scalar)
         turn_x(0, 0)
-        sort_u(1, 0)
+        interleave_x(1, 0, low)
         passes(1, 0, True)
-        turn_u(1, 0)
-        turn_x(1, 0)
-        interleave_x(1, 0)
-        sort_u(1, 1)
+        sort_u(1, 0)
         quantize_x_rows(1, 0)
-        quantize_u(1, 0)
-        turn_u(1, 1)
+        turn_u(1, 0)
+        sort_u(1, 1)
         passes(1, 1, True)
-        passes(1, 0, False)
         sort_u(0, 0)
-        sort_u(0, 1)
-        quantize_u(1, 1)
+        turn_u(1, 1)
         turn_u(0, 0)
+        quantize_u(1, 0)
+        sort_u(0, 1)
+        passes(1, 0, False)
+        interleave_x(0, 1, low)
+        quantize_u(1, 1)
         turn_u(0, 1)
-        interleave_x(0, 1)
+        sort_x(1, 0)
         quantize_u(0, 0)
         for b in range(4):
             first_pass(b, 1, 1, False)
-            residual(b, 1)
-        quantize_x_rows(0, 1)
+            residual(b, 1, on_scalar if b % 2 else on_vector)
         quantize_u(0, 1)
+        turn_x(1, 0)
+        interleave_x(0, 1, high)
         sort_x(0, 1)
         first_stage(0, 0)
-        interleave_x(1, 1)
+        quantize_x_rows(0, 1)
         first_stage(1, 0)
         turn_r(0, 1)
         turn_r(1, 1)
         turn_x(0, 1)
-        quantize_x_rows(1, 1)
         sort_x(1, 1)
+        interleave_x(1, 1)
         first_stage(2, 0)
-        quantize_x_cols(0, 0)
-        quantize_r(0, 1)
+        quantize_x_rows(1, 1)
         first_stage(3, 0)
         turn_r(0, 0)
         turn_x(1, 1)
-        quantize_r(1, 1)
+        quantize_x_cols(0, 0)
+        quantize_r(0, 1)
         quantize_x_cols(0, 1)
         nc.vector.tensor_scalar(out=dc_neg[:], in0=dc_raw[:], scalar1=-1.0, scalar2=None, op0=ALU.mult)
         first_stage(4, 0)
-        turn_r(1, 0)
         quantize_r(0, 0)
         quantize_x_cols(1, 0)
         first_stage(5, 0)
-        quantize_r(1, 0)
+        turn_r(1, 0)
         quantize_x_cols(1, 1)
-        second_pair(0, 0)
+        quantize_r(1, 1)
+        second(0, 0)
+        second(1, 0)
+        quantize_r(1, 0)
         first_stage(4, 1)
+        second_stage(2, 0)
+        second_stage(3, 0)
         turn_r(2, 0)
-        turn_y(0, 0)
-        second_pair(1, 0)
-        quantize_r(2, 0)
+        round_y(2, 0)
+        round_y(3, 0)
         first_stage(5, 1)
-        quantize_y(0, 0)
-        first_stage(6, 0)
-        turn_y(1, 0)
-        turn_r(2, 1)
-        first_stage(7, 0)
-        quantize_y(1, 0)
-        quantize_r(2, 1)
-        second_pair(2, 0)
+        quantize_r(2, 0)
+        second(0, 1)
+        second(1, 1)
         first_stage(6, 1)
-        turn_r(3, 0)
-        turn_y(2, 0)
+        turn_r(2, 1)
+        second(2, 1)
+        quantize_r(2, 1)
+        second_stage(3, 1)
         first_stage(7, 1)
-        quantize_r(3, 0)
-        second_stage(3, 0, 0)
-        second_stage(3, 1, 0)
+        round_y(3, 1)
+        turn_y(0, 0)
+        turn_y(1, 0)
+        first_stage(6, 0)
+        quantize_y(0, 0)
         turn_r(3, 1)
-        quantize_y(2, 0)
-        round_y(3, 0, 0)
-        round_y(3, 1, 0, True)
+        turn_y(2, 0)
+        quantize_y(1, 0)
         quantize_r(3, 1)
-        for hp in both:
-            for e in both:
-                second_pass(hp, e, 1, 0)
+        first_stage(7, 0)
+        quantize_y(2, 0)
+        second_stage(0, 2)
+        second_stage(1, 2)
+        turn_r(3, 0)
         turn_y(3, 0)
-        second_pair(0, 1)
-        second_pair(1, 1)
-        second_stage(2, 0, 1)
-        second_stage(2, 1, 1)
+        quantize_r(3, 0)
+        round_y(0, 2)
+        second_stage(2, 2)
+        round_y(1, 2)
+        second_stage(3, 2)
+        round_y(2, 2)
+        round_y(3, 2)
+        second(0, 3)
+        second(1, 3)
+        second_stage(2, 3)
+        second_stage(3, 3)
+        round_y(2, 3)
         turn_y(0, 1)
-        round_y(2, 0, 1)
-        second_stage(3, 0, 1)
-        second_stage(3, 1, 1)
-        turn_y(1, 1)
-        round_y(2, 1, 1, True)
-        round_y(3, 0, 1)
-        round_y(3, 1, 1, True)
         quantize_y(3, 0)
+        round_y(3, 3, on_vector)
+        turn_y(1, 1)
         quantize_y(0, 1)
-        turn_y(2, 1)
-        quantize_y(1, 1)
+        turn_y(2, 1, on_vector)
         turn_y(3, 1)
-        quantize_y(2, 1)
-        quantize_y(3, 1)
+        for hp in range(1, 4):
+            quantize_y(hp, 1)
         store_y_scales()

@@ -39,25 +39,26 @@ def tile_newton_inverse_refinement_k6_kernel(tc, b_words, b_scales, U, X, d_c, d
         x_raw = {(g, c): kept("x_raw%d%d" % (g, c), [P, 4, HALF], BF16) for g in both for c in both}
         u_raw = {(ih, g): kept("u_raw%d%d" % (ih, g), [P, 4, HALF], BF16) for ih in both for g in both}
         b_codes = {ih: kept("b_codes%d" % ih, [P, 2, 2 * HALF], U8) for ih in both}
-        b_plane = kept("b_plane", [P, 2, N], U8)
+        b_plane = {ih: kept("b_plane%d" % ih, [P, 2, HALF], U8) for ih in both}
         x_rows = {(g, c): mx_operand("x_rows%d%d" % (g, c), HALF) for g in both for c in both}
         x_cols = {(g, c): mx_operand("x_cols%d%d" % (g, c), HALF) for g in both for c in both}
         u_mx = {(ih, g): mx_operand("u_mx%d%d" % (ih, g), HALF) for ih in both for g in both}
         r_mx = {(jq, ih): mx_operand("r_mx%d%d" % (jq, ih), PAIR) for jq in range(4) for ih in both}
-        y_scales = kept("y_scales", [P, 2, N], U8)
+        y_scales = {jh: kept("y_scales%d" % jh, [P, N], U8) for jh in both}
         ident = kept("ident", [P, P], F32)
         two_eye = kept("two_eye", [P, 2, 224, 2], BF16)
         dc_raw = kept("dc_raw", [P, 4, 2], BF16)
         dc_neg = kept("dc_neg", [P, 4, 2], F32)
         dr_rows = kept("dr_rows", [P, N], BF16)
 
-        nc.vector.memset(b_plane[:].rearrange("p g n -> p (g n)").bitcast(I32), 0)
+        for ih in (1, 0):
+            nc.vector.memset(b_plane[ih][:].rearrange("p g n -> p (g n)").bitcast(I32), 0)
         make_identity(nc, ident[:])
-        nc.gpsimd.memset(two_eye[:], 0.0)
-        nc.gpsimd.tensor_scalar(
+        nc.vector.memset(two_eye[:], 0.0)
+        nc.vector.tensor_scalar(
             out=two_eye[:, :, 96:128, :],
             in0=ident[:].rearrange("p (w u e) -> p u w e", u=2, e=2),
-            scalar1=2.0, scalar2=0.0, op0=ALU.mult, op1=ALU.add,
+            scalar1=2.0, scalar2=None, op0=ALU.mult,
         )
 
         def load_x(g, c):
@@ -71,23 +72,20 @@ def tile_newton_inverse_refinement_k6_kernel(tc, b_words, b_scales, U, X, d_c, d
         def load_b(ih):
             src = b_words[:, :, ih * 2 * HALF:(ih + 1) * 2 * HALF].bitcast(I32)
             nc.sync.dma_start(out=b_codes[ih][:].bitcast(I32), in_=src.rearrange("g p n -> p g n"))
-
-        def load_b_scales():
             for q in range(4):
+                rows = b_scales[:, 4 * q:4 * q + 4, ih * HALF:(ih + 1) * HALF].bitcast(I32)
                 nc.sync.dma_start(
-                    out=b_plane[32 * q:32 * q + 4, :, :].bitcast(I32),
-                    in_=b_scales[:, 4 * q:4 * q + 4, :].bitcast(I32).rearrange("g r n -> r g n"),
+                    out=b_plane[ih][32 * q:32 * q + 4, :, :].bitcast(I32), in_=rows.rearrange("g r n -> r g n")
                 )
 
         load_x(0, 0)
         load_b(1)
-        load_b_scales()
         load_x(1, 0)
         load_u(1, 0)
         load_u(1, 1)
         load_u(0, 0)
-        load_b(0)
         load_u(0, 1)
+        load_b(0)
         load_x(0, 1)
         load_x(1, 1)
         nc.sync.dma_start(out=dc_raw[:], in_=d_c.rearrange("(a p e) -> p a e", p=P, e=2))
@@ -130,25 +128,22 @@ def tile_newton_inverse_refinement_k6_kernel(tc, b_words, b_scales, U, X, d_c, d
         def words(tile):
             return tile[:].rearrange("p c t -> p (c t)").bitcast(F32)
 
-        def sort_words(key, raw, on_vector=True):
+        def sort_words(key, raw, engine_copy):
             dst = flow.tile([P, 4, 2, P], F32, name="sorted_raw", bufs=4, align_bytes=64)
             sorted_raw[key] = dst
             src = raw[:].bitcast(F32).rearrange("p r (w u) -> p r u w", u=2)
-            if on_vector:
-                nc.vector.tensor_copy(out=dst[:], in_=src)
-            else:
-                nc.scalar.copy(out=dst[:], in_=src)
+            engine_copy(out=dst[:], in_=src)
 
         def word_class(key, raw, r, u):
             if key in sorted_raw:
                 return sorted_raw[key][:, r, u, :]
             return raw[:].bitcast(F32)[:, r, u:PAIR:2]
 
-        def sort_u(ih, g, on_vector=True):
-            sort_words(("u", ih, g), u_raw[ih, g], on_vector)
+        def sort_u(ih, g, engine_copy=nc.vector.tensor_copy):
+            sort_words(("u", ih, g), u_raw[ih, g], engine_copy)
 
-        def sort_x(g, c, on_vector=True):
-            sort_words(("x", g, c), x_raw[g, c], on_vector)
+        def sort_x(g, c, engine_copy=nc.vector.tensor_copy):
+            sort_words(("x", g, c), x_raw[g, c], engine_copy)
 
         def turn_u(ih, g):
             dst = staging(("u", ih, g), HALF)
@@ -182,7 +177,7 @@ def tile_newton_inverse_refinement_k6_kernel(tc, b_words, b_scales, U, X, d_c, d
             codes, scales = x_rows[g, b // 4]
             if base:
                 rhs = b_codes[ih][:, g, :].bitcast(FP4X4)
-                rhs_scale = b_plane[:, g, ih * HALF:(ih + 1) * HALF]
+                rhs_scale = b_plane[ih][:, g, :]
             else:
                 rhs = u_mx[ih, g][0][:].bitcast(FP8X4)
                 rhs_scale = u_mx[ih, g][1][:]
@@ -265,16 +260,15 @@ def tile_newton_inverse_refinement_k6_kernel(tc, b_words, b_scales, U, X, d_c, d
         def quantize_y(hp, jh):
             codes = flow.tile([P, PAIR], U32, name="y_codes", bufs=8, align_bytes=64)
             cols = slice(hp * PAIR, (hp + 1) * PAIR)
-            quantize(("y", hp, jh), codes[:], y_scales[:, jh, cols])
+            quantize(("y", hp, jh), codes[:], y_scales[jh][:, cols])
             dst = out_1[jh].rearrange("p m t -> p (m t)").bitcast(I32)
             nc.sync.dma_start(out=dst[:, cols], in_=codes[:].bitcast(I32))
 
-        def store_y_scales():
+        def store_y_scales(jh, queues=(nc.sync,)):
             for q in range(4):
-                queue = nc.scalar if q % 2 else nc.sync
-                queue.dma_start(
-                    out=out_2[:, 4 * q:4 * q + 4, :].bitcast(I32).rearrange("g r n -> r g n"),
-                    in_=y_scales[32 * q:32 * q + 4, :, :].bitcast(I32),
+                queues[q % len(queues)].dma_start(
+                    out=out_2[jh, 4 * q:4 * q + 4, :].bitcast(I32),
+                    in_=y_scales[jh][32 * q:32 * q + 4, :].bitcast(I32),
                 )
 
         on_vector = nc.vector.tensor_copy
@@ -305,17 +299,18 @@ def tile_newton_inverse_refinement_k6_kernel(tc, b_words, b_scales, U, X, d_c, d
         sort_u(0, 0)
         turn_u(1, 1)
         turn_u(0, 0)
+        quantize_x_cols(0, 0)
         quantize_u(1, 0)
         sort_u(0, 1)
+        sort_x(1, 0)
         passes(1, 0, False)
-        interleave_x(0, 1, low)
         quantize_u(1, 1)
         turn_u(0, 1)
-        sort_x(1, 0)
         quantize_u(0, 0)
         for b in range(4):
             first_pass(b, 1, 1, False)
-            residual(b, 1, on_scalar if b % 2 else on_vector)
+            residual(b, 1)
+        interleave_x(0, 1, low)
         quantize_u(0, 1)
         turn_x(1, 0)
         interleave_x(0, 1, high)
@@ -333,7 +328,6 @@ def tile_newton_inverse_refinement_k6_kernel(tc, b_words, b_scales, U, X, d_c, d
         first_stage(3, 0)
         turn_r(0, 0)
         turn_x(1, 1)
-        quantize_x_cols(0, 0)
         quantize_r(0, 1)
         quantize_x_cols(0, 1)
         nc.vector.tensor_scalar(out=dc_neg[:], in0=dc_raw[:], scalar1=-1.0, scalar2=None, op0=ALU.mult)
@@ -341,43 +335,43 @@ def tile_newton_inverse_refinement_k6_kernel(tc, b_words, b_scales, U, X, d_c, d
         quantize_r(0, 0)
         quantize_x_cols(1, 0)
         first_stage(5, 0)
-        turn_r(1, 0)
         quantize_x_cols(1, 1)
         quantize_r(1, 1)
         second(0, 0)
         second(1, 0)
-        quantize_r(1, 0)
         first_stage(4, 1)
         second_stage(2, 0)
         second_stage(3, 0)
+        turn_r(1, 0)
         turn_r(2, 0)
         round_y(2, 0)
         round_y(3, 0)
+        quantize_r(1, 0)
         first_stage(5, 1)
         quantize_r(2, 0)
+        first_stage(6, 1)
         second(0, 1)
         second(1, 1)
-        first_stage(6, 1)
-        turn_r(2, 1)
-        second(2, 1)
-        quantize_r(2, 1)
-        second_stage(3, 1)
         first_stage(7, 1)
-        round_y(3, 1)
+        second(2, 1)
+        second_stage(3, 1)
+        turn_r(2, 1)
         turn_y(0, 0)
-        turn_y(1, 0)
-        first_stage(6, 0)
-        quantize_y(0, 0)
+        turn_y(1, 0, on_vector)
         turn_r(3, 1)
-        turn_y(2, 0)
+        round_y(3, 1, on_vector)
+        first_stage(6, 0)
+        quantize_r(2, 1)
+        quantize_y(0, 0)
         quantize_y(1, 0)
         quantize_r(3, 1)
+        turn_y(2, 0, on_vector)
         first_stage(7, 0)
-        quantize_y(2, 0)
         second_stage(0, 2)
         second_stage(1, 2)
         turn_r(3, 0)
         turn_y(3, 0)
+        quantize_y(2, 0)
         quantize_r(3, 0)
         round_y(0, 2)
         second_stage(2, 2)
@@ -392,6 +386,7 @@ def tile_newton_inverse_refinement_k6_kernel(tc, b_words, b_scales, U, X, d_c, d
         round_y(2, 3)
         turn_y(0, 1)
         quantize_y(3, 0)
+        store_y_scales(0)
         round_y(3, 3, on_vector)
         turn_y(1, 1)
         quantize_y(0, 1)
@@ -399,4 +394,4 @@ def tile_newton_inverse_refinement_k6_kernel(tc, b_words, b_scales, U, X, d_c, d
         turn_y(3, 1)
         for hp in range(1, 4):
             quantize_y(hp, 1)
-        store_y_scales()
+        store_y_scales(1, (nc.sync, nc.scalar))

@@ -16,18 +16,28 @@ FP4X4 = mybir.dt.float4_e2m1fn_x4
 ALU = mybir.AluOpType
 
 P = 128
+PACK = 4
 HALF = 512
-PAIR = 256
+QUARTER = 256
+BOTH = (0, 1)
+BLOCKS_PER_HALF = HALF // P
+ACC_BANKS = 4
+TURN_BANKS = 4
+DEPTH = 8
+SORT_DEPTH = 4
+EYE_AT = 96
 
 
 def tile_newton_inverse_refinement_k6_kernel(tc, b_words, b_scales, U, X, d_c, d_r, out_0, out_1, out_2):
     nc = tc.nc
     with ExitStack() as ctx:
         keep = ctx.enter_context(tc.tile_pool(name="keep", bufs=1))
-        flow = ctx.enter_context(tc.tile_pool(name="flow", bufs=4))
-        acc_pool = ctx.enter_context(tc.psum_pool(name="acc", bufs=4))
-        turn_pool = ctx.enter_context(tc.psum_pool(name="turn", bufs=4))
+        flow = ctx.enter_context(tc.tile_pool(name="flow", bufs=DEPTH))
+        acc_pool = ctx.enter_context(tc.psum_pool(name="acc", bufs=ACC_BANKS))
+        turn_pool = ctx.enter_context(tc.psum_pool(name="turn", bufs=TURN_BANKS))
         ctx.enter_context(tc.manual_schedule())
+        on_vector = nc.vector.tensor_copy
+        on_scalar = nc.scalar.copy
 
         def kept(name, shape, dtype):
             return keep.tile(shape, dtype, name=name, align_bytes=64)
@@ -35,18 +45,17 @@ def tile_newton_inverse_refinement_k6_kernel(tc, b_words, b_scales, U, X, d_c, d
         def mx_operand(name, width):
             return kept(name + "_codes", [P, width], U32), kept(name + "_scales", [P, width], U8)
 
-        both = (0, 1)
-        x_raw = {(g, c): kept("x_raw%d%d" % (g, c), [P, 4, HALF], BF16) for g in both for c in both}
-        u_raw = {(ih, g): kept("u_raw%d%d" % (ih, g), [P, 4, HALF], BF16) for ih in both for g in both}
-        b_codes = {ih: kept("b_codes%d" % ih, [P, 2, 2 * HALF], U8) for ih in both}
-        b_plane = {ih: kept("b_plane%d" % ih, [P, 2, HALF], U8) for ih in both}
-        x_rows = {(g, c): mx_operand("x_rows%d%d" % (g, c), HALF) for g in both for c in both}
-        x_cols = {(g, c): mx_operand("x_cols%d%d" % (g, c), HALF) for g in both for c in both}
-        u_mx = {(ih, g): mx_operand("u_mx%d%d" % (ih, g), HALF) for ih in both for g in both}
-        r_mx = {(jq, ih): mx_operand("r_mx%d%d" % (jq, ih), PAIR) for jq in range(4) for ih in both}
-        y_scales = {jh: kept("y_scales%d" % jh, [P, N], U8) for jh in both}
+        x_raw = {(g, c): kept("x_raw%d%d" % (g, c), [P, PACK, HALF], BF16) for g in BOTH for c in BOTH}
+        u_raw = {(ih, g): kept("u_raw%d%d" % (ih, g), [P, BLOCKS_PER_HALF, HALF], BF16) for ih in BOTH for g in BOTH}
+        b_codes = {ih: kept("b_codes%d" % ih, [P, 2, 2 * HALF], U8) for ih in BOTH}
+        b_plane = {ih: kept("b_plane%d" % ih, [P, 2, HALF], U8) for ih in BOTH}
+        x_rows = {(g, c): mx_operand("x_rows%d%d" % (g, c), HALF) for g in BOTH for c in BOTH}
+        x_cols = {(g, c): mx_operand("x_cols%d%d" % (g, c), HALF) for g in BOTH for c in BOTH}
+        u_mx = {(ih, g): mx_operand("u_mx%d%d" % (ih, g), HALF) for ih in BOTH for g in BOTH}
+        r_mx = {(jq, ih): mx_operand("r_mx%d%d" % (jq, ih), QUARTER) for jq in range(4) for ih in BOTH}
+        y_scales = {jh: kept("y_scales%d" % jh, [P, N], U8) for jh in BOTH}
         ident = kept("ident", [P, P], F32)
-        two_eye = kept("two_eye", [P, 2, 224, 2], BF16)
+        two_eye = kept("two_eye", [P, 2, EYE_AT + P, 2], BF16)
         dc_raw = kept("dc_raw", [P, 4, 2], BF16)
         dc_neg = kept("dc_neg", [P, 4, 2], F32)
         dr_rows = kept("dr_rows", [P, N], BF16)
@@ -56,14 +65,14 @@ def tile_newton_inverse_refinement_k6_kernel(tc, b_words, b_scales, U, X, d_c, d
         make_identity(nc, ident[:])
         nc.vector.memset(two_eye[:], 0.0)
         nc.vector.tensor_scalar(
-            out=two_eye[:, :, 96:128, :],
+            out=two_eye[:, :, EYE_AT:P, :],
             in0=ident[:].rearrange("p (w u e) -> p u w e", u=2, e=2),
             scalar1=2.0, scalar2=None, op0=ALU.mult,
         )
 
         def load_x(g, c):
             rows = X[g * HALF:(g + 1) * HALF, c * HALF:(c + 1) * HALF]
-            nc.sync.dma_start(out=x_raw[g, c][:], in_=rows.rearrange("(p t) n -> p t n", t=4))
+            nc.sync.dma_start(out=x_raw[g, c][:], in_=rows.rearrange("(p t) n -> p t n", t=PACK))
 
         def load_u(ih, g):
             rows = U[ih * HALF:(ih + 1) * HALF, g * HALF:(g + 1) * HALF]
@@ -81,36 +90,45 @@ def tile_newton_inverse_refinement_k6_kernel(tc, b_words, b_scales, U, X, d_c, d
         load_x(0, 0)
         load_b(1)
         load_x(1, 0)
-        load_u(1, 0)
-        load_u(1, 1)
-        load_u(0, 0)
-        load_u(0, 1)
+        for ih in (1, 0):
+            for g in BOTH:
+                load_u(ih, g)
         load_b(0)
-        load_x(0, 1)
-        load_x(1, 1)
+        for g in BOTH:
+            load_x(g, 1)
         nc.sync.dma_start(out=dc_raw[:], in_=d_c.rearrange("(a p e) -> p a e", p=P, e=2))
         nc.sync.dma_start(out=dr_rows[:], in_=d_r.partition_broadcast(P))
 
         grouped = {}
-        accs = {}
-        r_turned = {}
-        y_sorted = {}
-        ys = {}
         sorted_raw = {}
+        p_banks = {}
+        r_sorted = {}
+        y_f32 = {}
+        y_sorted = {}
 
         def staging(key, width):
             if key not in grouped:
-                grouped[key] = flow.tile([P, width, 4], BF16, name="grouped%d" % width, bufs=8, align_bytes=64)
+                grouped[key] = flow.tile([P, width, PACK], BF16, name="grouped%d" % width, align_bytes=64)
             return grouped[key]
+
+        def as_words(tile):
+            return tile[:].rearrange("p c t -> p (c t)").bitcast(F32)
 
         def quantize(key, codes, scales, cols=slice(None)):
             nc.vector.quantize_mx(
                 out=codes.bitcast(FP8X4), scales=scales, in_=grouped[key][:, cols, :].rearrange("p c t -> p (c t)")
             )
 
-        def interleave_x(g, c, cols=slice(0, HALF), engine_copy=nc.vector.tensor_copy):
+        def turn(sources):
+            bank = turn_pool.tile([P, 2, 2, P], F32, name="turn")
+            for a in BOTH:
+                for u in BOTH:
+                    nc.tensor.transpose(bank[:, a, u, :], sources(a, u), ident[:])
+            return bank
+
+        def interleave_x(g, c, cols=slice(0, HALF), copy=on_vector):
             dst = staging(("x_rows", g, c), HALF)
-            engine_copy(
+            copy(
                 out=dst[:, cols, :].rearrange("p (c i) t -> p c t i", i=4),
                 in_=x_raw[g, c][:, :, cols].rearrange("p t (c i) -> p c t i", i=4),
             )
@@ -118,51 +136,40 @@ def tile_newton_inverse_refinement_k6_kernel(tc, b_words, b_scales, U, X, d_c, d
         def quantize_x_rows(g, c, cols=slice(0, HALF)):
             quantize(("x_rows", g, c), x_rows[g, c][0][:, cols], x_rows[g, c][1][:, cols], cols)
 
-        def turn(sources):
-            bank = turn_pool.tile([P, 2, 2, P], F32, name="turn")
-            for a in both:
-                for u in both:
-                    nc.tensor.transpose(bank[:, a, u, :], sources(a, u), ident[:])
-            return bank
-
-        def words(tile):
-            return tile[:].rearrange("p c t -> p (c t)").bitcast(F32)
-
-        def sort_words(key, raw, engine_copy):
-            dst = flow.tile([P, 4, 2, P], F32, name="sorted_raw", bufs=4, align_bytes=64)
+        def sort_words(key, raw):
+            dst = flow.tile([P, 4, 2, P], F32, name="sorted_raw", bufs=SORT_DEPTH, align_bytes=64)
             sorted_raw[key] = dst
-            src = raw[:].bitcast(F32).rearrange("p r (w u) -> p r u w", u=2)
-            engine_copy(out=dst[:], in_=src)
+            on_vector(out=dst[:], in_=raw[:].bitcast(F32).rearrange("p r (w u) -> p r u w", u=2))
 
-        def word_class(key, raw, r, u):
-            if key in sorted_raw:
-                return sorted_raw[key][:, r, u, :]
-            return raw[:].bitcast(F32)[:, r, u:PAIR:2]
+        def sort_u(ih, g):
+            sort_words(("u", ih, g), u_raw[ih, g])
 
-        def sort_u(ih, g, engine_copy=nc.vector.tensor_copy):
-            sort_words(("u", ih, g), u_raw[ih, g], engine_copy)
-
-        def sort_x(g, c, engine_copy=nc.vector.tensor_copy):
-            sort_words(("x", g, c), x_raw[g, c], engine_copy)
+        def sort_x(g, c):
+            sort_words(("x", g, c), x_raw[g, c])
 
         def turn_u(ih, g):
             dst = staging(("u", ih, g), HALF)
-            for k in both:
-                bank = turn(lambda a, u: word_class(("u", ih, g), u_raw[ih, g], 2 * k + a, u))
-                nc.scalar.copy(
-                    out=words(dst)[:, k * HALF:(k + 1) * HALF].rearrange("p (a i u) -> p a i u", a=2, u=2),
+            for k in BOTH:
+                bank = turn(lambda a, u: sorted_raw["u", ih, g][:, 2 * k + a, u, :])
+                on_scalar(
+                    out=as_words(dst)[:, k * HALF:(k + 1) * HALF].rearrange("p (a i u) -> p a i u", a=2, u=2),
                     in_=bank[:].rearrange("p a u i -> p a i u"),
                 )
 
         def quantize_u(ih, g):
             quantize(("u", ih, g), u_mx[ih, g][0][:], u_mx[ih, g][1][:])
 
-        def turn_x(g, c, parities=both, engine_copy=nc.scalar.copy):
+        def x_words(g, c, t, u):
+            if ("x", g, c) in sorted_raw:
+                return sorted_raw["x", g, c][:, t, u, :]
+            return x_raw[g, c][:].bitcast(F32)[:, t, u:QUARTER:2]
+
+        def turn_x(g, c):
             dst = staging(("x_cols", g, c), HALF)
-            for e in parities:
-                bank = turn(lambda a, u: word_class(("x", g, c), x_raw[g, c], e + 2 * a, u))
-                engine_copy(
-                    out=words(dst).rearrange("p (s e q a u) -> p s e q a u", s=2, e=2, a=2, u=2)[:, :, e, :, :, :],
+            for e in BOTH:
+                bank = turn(lambda a, u: x_words(g, c, e + 2 * a, u))
+                on_scalar(
+                    out=as_words(dst).rearrange("p (s e q a u) -> p s e q a u", s=2, e=2, a=2, u=2)[:, :, e, :, :, :],
                     in_=bank[:].rearrange("p a u (s q) -> p s q a u", s=2),
                 )
 
@@ -170,11 +177,12 @@ def tile_newton_inverse_refinement_k6_kernel(tc, b_words, b_scales, U, X, d_c, d
             quantize(("x_cols", g, c), x_cols[g, c][0][:], x_cols[g, c][1][:])
 
         def first_pass(b, ih, g, base):
-            first = base and g == 0
-            if first:
-                accs[b, ih] = acc_pool.tile([P, HALF], F32, name="acc")
-            cols = slice(P * (b % 4), P * (b % 4 + 1))
-            codes, scales = x_rows[g, b // 4]
+            opens = base and g == 0
+            if opens:
+                p_banks[b, ih] = acc_pool.tile([P, HALF], F32, name="acc")
+            c, block = divmod(b, BLOCKS_PER_HALF)
+            cols = slice(P * block, P * (block + 1))
+            codes, scales = x_rows[g, c]
             if base:
                 rhs = b_codes[ih][:, g, :].bitcast(FP4X4)
                 rhs_scale = b_plane[ih][:, g, :]
@@ -182,107 +190,107 @@ def tile_newton_inverse_refinement_k6_kernel(tc, b_words, b_scales, U, X, d_c, d
                 rhs = u_mx[ih, g][0][:].bitcast(FP8X4)
                 rhs_scale = u_mx[ih, g][1][:]
             nc.tensor.matmul_mx(
-                out=accs[b, ih][:], lhsT=codes[:, cols].bitcast(FP8X4), lhsT_scale=scales[:, cols],
-                rhs=rhs, rhs_scale=rhs_scale, start=first, stop=(g == 1 and not base),
+                out=p_banks[b, ih][:], lhsT=codes[:, cols].bitcast(FP8X4), lhsT_scale=scales[:, cols],
+                rhs=rhs, rhs_scale=rhs_scale, start=opens, stop=(g == 1 and not base),
             )
 
-        def residual(b, ih, engine_copy=nc.scalar.copy):
-            dst = flow.tile([P, 2, P, 2], BF16, name="r_turned", bufs=8, align_bytes=64)
-            r_turned[b, ih] = dst
-            src = accs[b, ih][:].rearrange("p (w u e) -> p u w e", u=2, e=2)
-            if b // 4 == ih:
-                w0 = 96 - 32 * (b % 4)
+        def residual(b, ih):
+            dst = flow.tile([P, 2, P, 2], BF16, name="r_sorted", align_bytes=64)
+            r_sorted[b, ih] = dst
+            src = p_banks[b, ih][:].rearrange("p (w u e) -> p u w e", u=2, e=2)
+            c, block = divmod(b, BLOCKS_PER_HALF)
+            if c == ih:
+                w0 = EYE_AT - 32 * block
                 nc.vector.tensor_tensor(out=dst[:], in0=src, in1=two_eye[:, :, w0:w0 + P, :], op=ALU.subtract)
             else:
-                engine_copy(out=dst[:], in_=src)
+                on_scalar(out=dst[:], in_=src)
 
         def first_stage(b, ih):
             for base in (True, False):
-                for g in both:
+                for g in BOTH:
                     first_pass(b, ih, g, base)
             residual(b, ih)
 
-        def sorted_words(tile, u):
-            return tile.rearrange("p u w e -> p u (w e)").bitcast(F32)[:, u, :]
+        def first_passes(ih, g, base):
+            for b in range(ACC_BANKS):
+                first_pass(b, ih, g, base)
 
-        def turn_r(bp, ih):
-            dst = staging(("r", bp, ih), PAIR)
-            bank = turn(lambda a, u: sorted_words(r_turned[2 * bp + a, ih][:], u))
-            nc.scalar.copy(
-                out=words(dst).rearrange("p (a j u) -> p a j u", a=2, u=2),
+        def sorted_words(rows, u):
+            return rows.rearrange("p u w e -> p u (w e)").bitcast(F32)[:, u, :]
+
+        def turn_r(jq, ih):
+            dst = staging(("r", jq, ih), QUARTER)
+            bank = turn(lambda a, u: sorted_words(r_sorted[2 * jq + a, ih][:], u))
+            on_scalar(
+                out=as_words(dst).rearrange("p (a j u) -> p a j u", a=2, u=2),
                 in_=bank[:].rearrange("p a u j -> p a j u"),
             )
 
-        def quantize_r(bp, ih):
-            codes, scales = r_mx[bp, ih]
-            quantize(("r", bp, ih), codes[:], scales[:])
+        def quantize_r(jq, ih):
+            codes, scales = r_mx[jq, ih]
+            quantize(("r", jq, ih), codes[:], scales[:])
 
         def second_stage(hp, jq):
-            acc = acc_pool.tile([P, 2, PAIR], F32, name="acc")
-            for e in both:
-                c0 = PAIR * (hp % 2) + P * e
-                for ih in both:
-                    codes, scales = x_cols[hp // 2, ih]
+            g, s = divmod(hp, 2)
+            acc = acc_pool.tile([P, 2, QUARTER], F32, name="acc")
+            for e in BOTH:
+                c0 = QUARTER * s + P * e
+                for ih in BOTH:
+                    codes, scales = x_cols[g, ih]
                     nc.tensor.matmul_mx(
                         out=acc[:, e, :], lhsT=codes[:, c0:c0 + P].bitcast(FP8X4), lhsT_scale=scales[:, c0:c0 + P],
                         rhs=r_mx[jq, ih][0][:].bitcast(FP8X4), rhs_scale=r_mx[jq, ih][1][:],
                         start=(ih == 0), stop=(ih == 1),
                     )
-            cols = slice(jq * PAIR, (jq + 1) * PAIR)
-            y = flow.tile([P, 2, PAIR], F32, name="y", bufs=8, align_bytes=64)
-            ys[hp, jq] = y
-            for e in both:
+            cols = slice(jq * QUARTER, (jq + 1) * QUARTER)
+            y = flow.tile([P, 2, QUARTER], F32, name="y", align_bytes=64)
+            y_f32[hp, jq] = y
+            for e in BOTH:
                 nc.vector.scalar_tensor_tensor(
                     out=y[:, e, :], in0=acc[:, e, :], scalar=dc_neg[:, hp, e:e + 1], in1=dr_rows[:, cols],
                     op0=ALU.mult, op1=ALU.mult,
                 )
-            rows = out_0[hp * PAIR:(hp + 1) * PAIR, cols]
+            rows = out_0[hp * QUARTER:(hp + 1) * QUARTER, cols]
             nc.sync.dma_start(out=rows.rearrange("(p e) n -> p e n", e=2), in_=y[:])
 
-        def round_y(hp, jq, engine_copy=nc.scalar.copy):
-            jh = jq // 2
+        def round_y(hp, jq, copy=on_scalar):
+            jh, side = divmod(jq, 2)
             if (hp, jh) not in y_sorted:
-                y_sorted[hp, jh] = flow.tile([P, 2, 2, P, 2], BF16, name="y_sorted", bufs=8, align_bytes=64)
-            w0 = 64 * (jq % 2)
-            engine_copy(
+                y_sorted[hp, jh] = flow.tile([P, 2, 2, P, 2], BF16, name="y_sorted", align_bytes=64)
+            w0 = 64 * side
+            copy(
                 out=y_sorted[hp, jh][:, :, :, w0:w0 + 64, :],
-                in_=ys[hp, jq][:].rearrange("p e (w u f) -> p e u w f", u=2, f=2),
+                in_=y_f32[hp, jq][:].rearrange("p e (w u f) -> p e u w f", u=2, f=2),
             )
 
-        def turn_y(hp, jh, engine_copy=nc.scalar.copy):
-            dst = staging(("y", hp, jh), PAIR)
+        def second_and_round(hp, jq):
+            second_stage(hp, jq)
+            round_y(hp, jq)
+
+        def turn_y(hp, jh, copy=on_scalar):
+            dst = staging(("y", hp, jh), QUARTER)
             bank = turn(lambda a, u: sorted_words(y_sorted[hp, jh][:, a], u))
-            engine_copy(
-                out=words(dst).rearrange("p (m a u) -> p m a u", a=2, u=2),
+            copy(
+                out=as_words(dst).rearrange("p (m a u) -> p m a u", a=2, u=2),
                 in_=bank[:].rearrange("p a u m -> p m a u"),
             )
 
         def quantize_y(hp, jh):
-            codes = flow.tile([P, PAIR], U32, name="y_codes", bufs=8, align_bytes=64)
-            cols = slice(hp * PAIR, (hp + 1) * PAIR)
+            codes = flow.tile([P, QUARTER], U32, name="y_codes", align_bytes=64)
+            cols = slice(hp * QUARTER, (hp + 1) * QUARTER)
             quantize(("y", hp, jh), codes[:], y_scales[jh][:, cols])
             dst = out_1[jh].rearrange("p m t -> p (m t)").bitcast(I32)
             nc.sync.dma_start(out=dst[:, cols], in_=codes[:].bitcast(I32))
 
-        def store_y_scales(jh, queues=(nc.sync,)):
+        def store_y_scales(jh, queues):
             for q in range(4):
                 queues[q % len(queues)].dma_start(
                     out=out_2[jh, 4 * q:4 * q + 4, :].bitcast(I32),
                     in_=y_scales[jh][32 * q:32 * q + 4, :].bitcast(I32),
                 )
 
-        on_vector = nc.vector.tensor_copy
-        on_scalar = nc.scalar.copy
 
-        def passes(ih, g, base):
-            for b in range(4):
-                first_pass(b, ih, g, base)
-
-        def second(hp, jq):
-            second_stage(hp, jq)
-            round_y(hp, jq)
-
-        low, high = slice(0, PAIR), slice(PAIR, HALF)
+        low, high = slice(0, QUARTER), slice(QUARTER, HALF)
         interleave_x(0, 0, low)
         interleave_x(0, 0, high, on_scalar)
         quantize_x_rows(0, 0, low)
@@ -290,12 +298,12 @@ def tile_newton_inverse_refinement_k6_kernel(tc, b_words, b_scales, U, X, d_c, d
         interleave_x(1, 0, high, on_scalar)
         turn_x(0, 0)
         interleave_x(1, 0, low)
-        passes(1, 0, True)
+        first_passes(1, 0, True)
         sort_u(1, 0)
         quantize_x_rows(1, 0)
         turn_u(1, 0)
         sort_u(1, 1)
-        passes(1, 1, True)
+        first_passes(1, 1, True)
         sort_u(0, 0)
         turn_u(1, 1)
         turn_u(0, 0)
@@ -303,16 +311,17 @@ def tile_newton_inverse_refinement_k6_kernel(tc, b_words, b_scales, U, X, d_c, d
         quantize_u(1, 0)
         sort_u(0, 1)
         sort_x(1, 0)
-        passes(1, 0, False)
+        first_passes(1, 0, False)
         quantize_u(1, 1)
         turn_u(0, 1)
         quantize_u(0, 0)
-        for b in range(4):
+        for b in range(ACC_BANKS):
             first_pass(b, 1, 1, False)
             residual(b, 1)
         interleave_x(0, 1, low)
         quantize_u(0, 1)
         turn_x(1, 0)
+
         interleave_x(0, 1, high)
         sort_x(0, 1)
         first_stage(0, 0)
@@ -337,8 +346,9 @@ def tile_newton_inverse_refinement_k6_kernel(tc, b_words, b_scales, U, X, d_c, d
         first_stage(5, 0)
         quantize_x_cols(1, 1)
         quantize_r(1, 1)
-        second(0, 0)
-        second(1, 0)
+
+        second_and_round(0, 0)
+        second_and_round(1, 0)
         first_stage(4, 1)
         second_stage(2, 0)
         second_stage(3, 0)
@@ -350,11 +360,12 @@ def tile_newton_inverse_refinement_k6_kernel(tc, b_words, b_scales, U, X, d_c, d
         first_stage(5, 1)
         quantize_r(2, 0)
         first_stage(6, 1)
-        second(0, 1)
-        second(1, 1)
+        second_and_round(0, 1)
+        second_and_round(1, 1)
         first_stage(7, 1)
-        second(2, 1)
+        second_and_round(2, 1)
         second_stage(3, 1)
+
         turn_r(2, 1)
         turn_y(0, 0)
         turn_y(1, 0, on_vector)
@@ -366,12 +377,15 @@ def tile_newton_inverse_refinement_k6_kernel(tc, b_words, b_scales, U, X, d_c, d
         quantize_y(1, 0)
         quantize_r(3, 1)
         turn_y(2, 0, on_vector)
+        turn_y(3, 0)
+        quantize_y(2, 0)
         first_stage(7, 0)
+        quantize_y(3, 0)
+        store_y_scales(0, (nc.sync,))
+
         second_stage(0, 2)
         second_stage(1, 2)
         turn_r(3, 0)
-        turn_y(3, 0)
-        quantize_y(2, 0)
         quantize_r(3, 0)
         round_y(0, 2)
         second_stage(2, 2)
@@ -379,14 +393,13 @@ def tile_newton_inverse_refinement_k6_kernel(tc, b_words, b_scales, U, X, d_c, d
         second_stage(3, 2)
         round_y(2, 2)
         round_y(3, 2)
-        second(0, 3)
-        second(1, 3)
+        second_and_round(0, 3)
+        second_and_round(1, 3)
         second_stage(2, 3)
         second_stage(3, 3)
         round_y(2, 3)
+
         turn_y(0, 1)
-        quantize_y(3, 0)
-        store_y_scales(0)
         round_y(3, 3, on_vector)
         turn_y(1, 1)
         quantize_y(0, 1)

from contextlib import ExitStack

import concourse.mybir as mybir
from concourse.masks import make_identity

N = 1024
FLOPS = 3 * 2 * N * N * N

F32 = mybir.dt.float32
BF16 = mybir.dt.bfloat16
I32 = mybir.dt.int32
U32 = mybir.dt.uint32
U8 = mybir.dt.uint8
FP8X4 = mybir.dt.float8_e4m3fn_x4
FP4X4 = mybir.dt.float4_e2m1fn_x4
ALU = mybir.AluOpType

P = 128
PACK = 4
HALF = 512
QUARTER = 256
BOTH = (0, 1)
BLOCKS_PER_HALF = HALF // P
ACC_BANKS = 4
TURN_BANKS = 4
DEPTH = 8
SORT_DEPTH = 4
EYE_AT = 96


def tile_newton_inverse_refinement_k6_kernel(tc, b_words, b_scales, U, X, d_c, d_r, out_0, out_1, out_2):
    nc = tc.nc
    with ExitStack() as ctx:
        keep = ctx.enter_context(tc.tile_pool(name="keep", bufs=1))
        flow = ctx.enter_context(tc.tile_pool(name="flow", bufs=DEPTH))
        acc_pool = ctx.enter_context(tc.psum_pool(name="acc", bufs=ACC_BANKS))
        turn_pool = ctx.enter_context(tc.psum_pool(name="turn", bufs=TURN_BANKS))
        ctx.enter_context(tc.manual_schedule())
        on_vector = nc.vector.tensor_copy
        on_scalar = nc.scalar.copy

        def kept(name, shape, dtype):
            return keep.tile(shape, dtype, name=name, align_bytes=64)

        def mx_operand(name, width):
            return kept(name + "_codes", [P, width], U32), kept(name + "_scales", [P, width], U8)

        x_raw = {(g, c): kept("x_raw%d%d" % (g, c), [P, PACK, HALF], BF16) for g in BOTH for c in BOTH}
        u_raw = {(ih, g): kept("u_raw%d%d" % (ih, g), [P, BLOCKS_PER_HALF, HALF], BF16) for ih in BOTH for g in BOTH}
        b_codes = {ih: kept("b_codes%d" % ih, [P, 2, 2 * HALF], U8) for ih in BOTH}
        b_plane = {ih: kept("b_plane%d" % ih, [P, 2, HALF], U8) for ih in BOTH}
        x_rows = {(g, c): mx_operand("x_rows%d%d" % (g, c), HALF) for g in BOTH for c in BOTH}
        x_cols = {(g, c): mx_operand("x_cols%d%d" % (g, c), HALF) for g in BOTH for c in BOTH}
        u_mx = {(ih, g): mx_operand("u_mx%d%d" % (ih, g), HALF) for ih in BOTH for g in BOTH}
        r_mx = {(jq, ih): mx_operand("r_mx%d%d" % (jq, ih), QUARTER) for jq in range(4) for ih in BOTH}
        y_scales = {jh: kept("y_scales%d" % jh, [P, N], U8) for jh in BOTH}
        ident = kept("ident", [P, P], F32)
        two_eye = kept("two_eye", [P, 2, EYE_AT + P, 2], BF16)
        dc_raw = kept("dc_raw", [P, 4, 2], BF16)
        dc_neg = kept("dc_neg", [P, 4, 2], F32)
        dr_rows = kept("dr_rows", [P, N], BF16)

        for ih in (1, 0):
            nc.vector.memset(b_plane[ih][:].rearrange("p g n -> p (g n)").bitcast(I32), 0)
        make_identity(nc, ident[:])
        nc.vector.memset(two_eye[:], 0.0)
        nc.vector.tensor_scalar(
            out=two_eye[:, :, EYE_AT:P, :],
            in0=ident[:].rearrange("p (w u e) -> p u w e", u=2, e=2),
            scalar1=2.0, scalar2=None, op0=ALU.mult,
        )

        def load_x(g, c):
            rows = X[g * HALF:(g + 1) * HALF, c * HALF:(c + 1) * HALF]
            nc.sync.dma_start(out=x_raw[g, c][:], in_=rows.rearrange("(p t) n -> p t n", t=PACK))

        def load_u(ih, g):
            rows = U[ih * HALF:(ih + 1) * HALF, g * HALF:(g + 1) * HALF]
            nc.sync.dma_start(out=u_raw[ih, g][:], in_=rows.rearrange("(r p) n -> p r n", p=P))

        def load_b(ih):
            src = b_words[:, :, ih * 2 * HALF:(ih + 1) * 2 * HALF].bitcast(I32)
            nc.sync.dma_start(out=b_codes[ih][:].bitcast(I32), in_=src.rearrange("g p n -> p g n"))
            for q in range(4):
                rows = b_scales[:, 4 * q:4 * q + 4, ih * HALF:(ih + 1) * HALF].bitcast(I32)
                nc.sync.dma_start(
                    out=b_plane[ih][32 * q:32 * q + 4, :, :].bitcast(I32), in_=rows.rearrange("g r n -> r g n")
                )

        load_x(0, 0)
        load_b(1)
        load_x(1, 0)
        for ih in (1, 0):
            for g in BOTH:
                load_u(ih, g)
        load_b(0)
        for g in BOTH:
            load_x(g, 1)
        nc.sync.dma_start(out=dc_raw[:], in_=d_c.rearrange("(a p e) -> p a e", p=P, e=2))
        nc.sync.dma_start(out=dr_rows[:], in_=d_r.partition_broadcast(P))

        grouped = {}
        sorted_raw = {}
        p_banks = {}
        r_sorted = {}
        y_f32 = {}
        y_sorted = {}

        def staging(key, width):
            if key not in grouped:
                grouped[key] = flow.tile([P, width, PACK], BF16, name="grouped%d" % width, align_bytes=64)
            return grouped[key]

        def as_words(tile):
            return tile[:].rearrange("p c t -> p (c t)").bitcast(F32)

        def quantize(key, codes, scales, cols=slice(None)):
            nc.vector.quantize_mx(
                out=codes.bitcast(FP8X4), scales=scales, in_=grouped[key][:, cols, :].rearrange("p c t -> p (c t)")
            )

        def turn(sources):
            bank = turn_pool.tile([P, 2, 2, P], F32, name="turn")
            for a in BOTH:
                for u in BOTH:
                    nc.tensor.transpose(bank[:, a, u, :], sources(a, u), ident[:])
            return bank

        def interleave_x(g, c, cols=slice(0, HALF), copy=on_vector):
            dst = staging(("x_rows", g, c), HALF)
            copy(
                out=dst[:, cols, :].rearrange("p (c i) t -> p c t i", i=4),
                in_=x_raw[g, c][:, :, cols].rearrange("p t (c i) -> p c t i", i=4),
            )

        def quantize_x_rows(g, c, cols=slice(0, HALF)):
            quantize(("x_rows", g, c), x_rows[g, c][0][:, cols], x_rows[g, c][1][:, cols], cols)

        def sort_words(key, raw):
            dst = flow.tile([P, 4, 2, P], F32, name="sorted_raw", bufs=SORT_DEPTH, align_bytes=64)
            sorted_raw[key] = dst
            on_vector(out=dst[:], in_=raw[:].bitcast(F32).rearrange("p r (w u) -> p r u w", u=2))

        def sort_u(ih, g):
            sort_words(("u", ih, g), u_raw[ih, g])

        def sort_x(g, c):
            sort_words(("x", g, c), x_raw[g, c])

        def turn_u(ih, g):
            dst = staging(("u", ih, g), HALF)
            for k in BOTH:
                bank = turn(lambda a, u: sorted_raw["u", ih, g][:, 2 * k + a, u, :])
                on_scalar(
                    out=as_words(dst)[:, k * HALF:(k + 1) * HALF].rearrange("p (a i u) -> p a i u", a=2, u=2),
                    in_=bank[:].rearrange("p a u i -> p a i u"),
                )

        def quantize_u(ih, g):
            quantize(("u", ih, g), u_mx[ih, g][0][:], u_mx[ih, g][1][:])

        def x_words(g, c, t, u):
            if ("x", g, c) in sorted_raw:
                return sorted_raw["x", g, c][:, t, u, :]
            return x_raw[g, c][:].bitcast(F32)[:, t, u:QUARTER:2]

        def turn_x(g, c):
            dst = staging(("x_cols", g, c), HALF)
            for e in BOTH:
                bank = turn(lambda a, u: x_words(g, c, e + 2 * a, u))
                on_scalar(
                    out=as_words(dst).rearrange("p (s e q a u) -> p s e q a u", s=2, e=2, a=2, u=2)[:, :, e, :, :, :],
                    in_=bank[:].rearrange("p a u (s q) -> p s q a u", s=2),
                )

        def quantize_x_cols(g, c):
            quantize(("x_cols", g, c), x_cols[g, c][0][:], x_cols[g, c][1][:])

        def first_pass(b, ih, g, base):
            opens = base and g == 0
            if opens:
                p_banks[b, ih] = acc_pool.tile([P, HALF], F32, name="acc")
            c, block = divmod(b, BLOCKS_PER_HALF)
            cols = slice(P * block, P * (block + 1))
            codes, scales = x_rows[g, c]
            if base:
                rhs = b_codes[ih][:, g, :].bitcast(FP4X4)
                rhs_scale = b_plane[ih][:, g, :]
            else:
                rhs = u_mx[ih, g][0][:].bitcast(FP8X4)
                rhs_scale = u_mx[ih, g][1][:]
            nc.tensor.matmul_mx(
                out=p_banks[b, ih][:], lhsT=codes[:, cols].bitcast(FP8X4), lhsT_scale=scales[:, cols],
                rhs=rhs, rhs_scale=rhs_scale, start=opens, stop=(g == 1 and not base),
            )

        def residual(b, ih):
            dst = flow.tile([P, 2, P, 2], BF16, name="r_sorted", align_bytes=64)
            r_sorted[b, ih] = dst
            src = p_banks[b, ih][:].rearrange("p (w u e) -> p u w e", u=2, e=2)
            c, block = divmod(b, BLOCKS_PER_HALF)
            if c == ih:
                w0 = EYE_AT - 32 * block
                nc.vector.tensor_tensor(out=dst[:], in0=src, in1=two_eye[:, :, w0:w0 + P, :], op=ALU.subtract)
            else:
                on_scalar(out=dst[:], in_=src)

        def first_stage(b, ih):
            for base in (True, False):
                for g in BOTH:
                    first_pass(b, ih, g, base)
            residual(b, ih)

        def first_passes(ih, g, base):
            for b in range(ACC_BANKS):
                first_pass(b, ih, g, base)

        def sorted_words(rows, u):
            return rows.rearrange("p u w e -> p u (w e)").bitcast(F32)[:, u, :]

        def turn_r(jq, ih):
            dst = staging(("r", jq, ih), QUARTER)
            bank = turn(lambda a, u: sorted_words(r_sorted[2 * jq + a, ih][:], u))
            on_scalar(
                out=as_words(dst).rearrange("p (a j u) -> p a j u", a=2, u=2),
                in_=bank[:].rearrange("p a u j -> p a j u"),
            )

        def quantize_r(jq, ih):
            codes, scales = r_mx[jq, ih]
            quantize(("r", jq, ih), codes[:], scales[:])

        def second_stage(hp, jq):
            g, s = divmod(hp, 2)
            acc = acc_pool.tile([P, 2, QUARTER], F32, name="acc")
            for e in BOTH:
                c0 = QUARTER * s + P * e
                for ih in BOTH:
                    codes, scales = x_cols[g, ih]
                    nc.tensor.matmul_mx(
                        out=acc[:, e, :], lhsT=codes[:, c0:c0 + P].bitcast(FP8X4), lhsT_scale=scales[:, c0:c0 + P],
                        rhs=r_mx[jq, ih][0][:].bitcast(FP8X4), rhs_scale=r_mx[jq, ih][1][:],
                        start=(ih == 0), stop=(ih == 1),
                    )
            cols = slice(jq * QUARTER, (jq + 1) * QUARTER)
            y = flow.tile([P, 2, QUARTER], F32, name="y", align_bytes=64)
            y_f32[hp, jq] = y
            for e in BOTH:
                nc.vector.scalar_tensor_tensor(
                    out=y[:, e, :], in0=acc[:, e, :], scalar=dc_neg[:, hp, e:e + 1], in1=dr_rows[:, cols],
                    op0=ALU.mult, op1=ALU.mult,
                )
            rows = out_0[hp * QUARTER:(hp + 1) * QUARTER, cols]
            nc.sync.dma_start(out=rows.rearrange("(p e) n -> p e n", e=2), in_=y[:])

        def round_y(hp, jq, copy=on_scalar):
            jh, side = divmod(jq, 2)
            if (hp, jh) not in y_sorted:
                y_sorted[hp, jh] = flow.tile([P, 2, 2, P, 2], BF16, name="y_sorted", align_bytes=64)
            w0 = 64 * side
            copy(
                out=y_sorted[hp, jh][:, :, :, w0:w0 + 64, :],
                in_=y_f32[hp, jq][:].rearrange("p e (w u f) -> p e u w f", u=2, f=2),
            )

        def second_and_round(hp, jq):
            second_stage(hp, jq)
            round_y(hp, jq)

        def turn_y(hp, jh, copy=on_scalar):
            dst = staging(("y", hp, jh), QUARTER)
            bank = turn(lambda a, u: sorted_words(y_sorted[hp, jh][:, a], u))
            copy(
                out=as_words(dst).rearrange("p (m a u) -> p m a u", a=2, u=2),
                in_=bank[:].rearrange("p a u m -> p m a u"),
            )

        def quantize_y(hp, jh):
            codes = flow.tile([P, QUARTER], U32, name="y_codes", align_bytes=64)
            cols = slice(hp * QUARTER, (hp + 1) * QUARTER)
            quantize(("y", hp, jh), codes[:], y_scales[jh][:, cols])
            dst = out_1[jh].rearrange("p m t -> p (m t)").bitcast(I32)
            nc.sync.dma_start(out=dst[:, cols], in_=codes[:].bitcast(I32))

        def store_y_scales(jh, queues):
            for q in range(4):
                queues[q % len(queues)].dma_start(
                    out=out_2[jh, 4 * q:4 * q + 4, :].bitcast(I32),
                    in_=y_scales[jh][32 * q:32 * q + 4, :].bitcast(I32),
                )


        low, high = slice(0, QUARTER), slice(QUARTER, HALF)
        interleave_x(0, 0, low)
        interleave_x(0, 0, high, on_scalar)
        quantize_x_rows(0, 0, low)
        quantize_x_rows(0, 0, high)
        interleave_x(1, 0, high, on_scalar)
        turn_x(0, 0)
        interleave_x(1, 0, low)
        first_passes(1, 0, True)
        sort_u(1, 0)
        quantize_x_rows(1, 0)
        turn_u(1, 0)
        sort_u(1, 1)
        first_passes(1, 1, True)
        sort_u(0, 0)
        turn_u(1, 1)
        turn_u(0, 0)
        quantize_x_cols(0, 0)
        quantize_u(1, 0)
        sort_u(0, 1)
        sort_x(1, 0)
        first_passes(1, 0, False)
        quantize_u(1, 1)
        turn_u(0, 1)
        quantize_u(0, 0)
        for b in range(ACC_BANKS):
            first_pass(b, 1, 1, False)
            residual(b, 1)
        interleave_x(0, 1, low)
        quantize_u(0, 1)
        turn_x(1, 0)

        interleave_x(0, 1, high)
        sort_x(0, 1)
        first_stage(0, 0)
        quantize_x_rows(0, 1)
        first_stage(1, 0)
        turn_r(0, 1)
        turn_r(1, 1)
        turn_x(0, 1)
        sort_x(1, 1)
        interleave_x(1, 1)
        first_stage(2, 0)
        quantize_x_rows(1, 1)
        first_stage(3, 0)
        turn_r(0, 0)
        turn_x(1, 1)
        quantize_r(0, 1)
        quantize_x_cols(0, 1)
        nc.vector.tensor_scalar(out=dc_neg[:], in0=dc_raw[:], scalar1=-1.0, scalar2=None, op0=ALU.mult)
        first_stage(4, 0)
        quantize_r(0, 0)
        quantize_x_cols(1, 0)
        first_stage(5, 0)
        quantize_x_cols(1, 1)
        quantize_r(1, 1)

        second_and_round(0, 0)
        second_and_round(1, 0)
        first_stage(4, 1)
        second_stage(2, 0)
        second_stage(3, 0)
        turn_r(1, 0)
        turn_r(2, 0)
        round_y(2, 0)
        round_y(3, 0)
        quantize_r(1, 0)
        first_stage(5, 1)
        quantize_r(2, 0)
        first_stage(6, 1)
        second_and_round(0, 1)
        second_and_round(1, 1)
        first_stage(7, 1)
        second_and_round(2, 1)
        second_stage(3, 1)

        turn_r(2, 1)
        turn_y(0, 0)
        turn_y(1, 0, on_vector)
        turn_r(3, 1)
        round_y(3, 1, on_vector)
        first_stage(6, 0)
        quantize_r(2, 1)
        quantize_y(0, 0)
        quantize_y(1, 0)
        quantize_r(3, 1)
        turn_y(2, 0, on_vector)
        turn_y(3, 0)
        quantize_y(2, 0)
        first_stage(7, 0)
        quantize_y(3, 0)
        store_y_scales(0, (nc.sync,))

        second_stage(0, 2)
        second_stage(1, 2)
        turn_r(3, 0)
        quantize_r(3, 0)
        round_y(0, 2)
        second_stage(2, 2)
        round_y(1, 2)
        second_stage(3, 2)
        round_y(2, 2)
        round_y(3, 2)
        second_and_round(0, 3)
        second_and_round(1, 3)
        second_stage(2, 3)
        second_stage(3, 3)
        round_y(2, 3)

        turn_y(0, 1)
        round_y(3, 3, on_vector)
        turn_y(1, 1)
        quantize_y(0, 1)
        turn_y(2, 1, on_vector)
        turn_y(3, 1)
        for hp in range(1, 4):
            quantize_y(hp, 1)
        store_y_scales(1, (nc.sync, nc.scalar))
